import numpy as np
import ml_dtypes


def mxq(x, axis, fmt="e4m3"):
    dtype, down = {"e4m3": (ml_dtypes.float8_e4m3fn, 7), "e5m2": (ml_dtypes.float8_e5m2, 14)}[fmt]
    v = np.moveaxis(np.asarray(x, np.float32).astype(ml_dtypes.bfloat16).astype(np.float64), axis, -1)
    blocks = v.reshape(v.shape[:-1] + (-1, 32))
    amax = np.abs(blocks).max(-1, keepdims=True)
    byte = np.maximum(np.where(amax > 0, np.frexp(amax)[1] - 1 + 127, 0) - down, 1)
    scale = np.exp2(byte - 127.0)
    codes = (blocks / scale).astype(np.float32).astype(dtype).astype(np.float64)
    return np.moveaxis((codes * scale).reshape(v.shape), -1, axis)


WIDE = False


def mx_kscale(k):
    if not WIDE:
        return np.ones(k)
    levels = np.array([10, -10, 5, -5, 0])
    if k % 512:
        return np.exp2(np.random.permutation(np.resize(levels, k // 32))).repeat(32)
    a = np.empty((k // 512, 16))
    for p in range(k // 512):
        a[p, :8] = np.random.permutation(np.resize(levels, 8))
        for g in range(8):
            far = levels[np.abs(levels - a[p, g]) >= 10]
            a[p, g + 8] = far[np.random.randint(len(far))]
    return np.exp2(a.ravel()).repeat(32)


def f64(x):
    return np.asarray(x).astype(np.float64)


def striped(idx):
    return np.tile(idx.reshape(-1, 16).T, (8, 1)).astype(np.uint16)


def unstriped(offs):
    return offs[:16].T.reshape(-1).astype(np.int64)


def striped8(idx):
    return np.concatenate([x.reshape(-1, 16).T for x in idx]).astype(np.uint16)


def runs(offs, k):
    lists = np.stack([offs[16 * r : 16 * r + 16].T.reshape(-1) for r in range(8)]).astype(np.int64)
    return lists[np.arange(k) % 512 // 64]


def pack_weight(w):
    k, n = w.shape
    w = f64(np.asarray(w, np.float32).astype(ml_dtypes.bfloat16)).reshape(k // 32, 32, n)
    amax = np.abs(w).max(1)
    byte = np.clip(np.where(amax > 0, np.frexp(amax)[1] - 1 + 127 - 7, 1), 1, 254)
    scaled = (w * np.exp2(127.0 - byte)[:, None, :]).reshape(k, n).astype(np.float32)
    words = np.ascontiguousarray(scaled.reshape(k // 512, 128, 4, n).transpose(0, 1, 3, 2)).astype(ml_dtypes.float8_e4m3fn).view(np.uint8)
    return words, np.ascontiguousarray(byte.astype(np.uint8).reshape(k // 512, 16, n))


def unpack_weight(words, scales):
    g, p, n, _ = words.shape
    vals = np.ascontiguousarray(words).view(ml_dtypes.float8_e4m3fn).astype(np.float64) * np.repeat(np.exp2(scales.astype(np.float64) - 127.0), 8, axis=1)[..., None]
    return vals.transpose(0, 1, 3, 2).reshape(g * 512, n)


def sigmoid(v):
    return 1.0 / (1.0 + np.exp(-np.maximum(v, -700.0)))


K, T, S, N, H = 512, 2048, 512, 512, 512


def setup_inputs():
    n = np.random.standard_normal
    s = mx_kscale(K)[:, None]
    u = mx_kscale(H)
    packed_xT = pack_weight(n((K, T)) * s)
    return {
        "x_words": packed_xT[0],
        "x_scales": packed_xT[1],
        "w1": (n((K, H)) / np.sqrt(K) / s).astype(np.float32),
        "gn": (np.random.uniform(0.5, 1.5, (H, 1)) * u[:, None]).astype(np.float32),
        "w2": (n((H, N)) / np.sqrt(H) / u[:, None]).astype(np.float32),
        "w3": (n((K, N)) / np.sqrt(K) / s).astype(np.float32),
        "offs": striped(np.random.permutation(T)[:S]),
        "n1": striped8(np.stack([np.random.permutation(S) for _ in range(8)])),
        "n2": striped8(np.stack([np.random.permutation(S) for _ in range(8)])),
        "two": striped(np.random.permutation(T)[:S]),
        "n3": striped8(np.stack([np.random.permutation(S) for _ in range(8)])),
        "n4": striped8(np.stack([np.random.permutation(S) for _ in range(8)])),
    }


def reference(x_words, x_scales, w1, gn, w2, w3, offs, n1, n2, two, n3, n4):
    xq = unpack_weight(x_words, x_scales)[:, unstriped(offs)]
    y = mxq(f64(w1), 0, "e4m3").T @ xq
    st = y + y[np.arange(H)[:, None], runs(n1, H)]
    z = f64(gn) * (st * (np.tanh(st[np.arange(H)[:, None], runs(n2, H)])))
    h = mxq(f64(w2), 0, "e4m3").T @ mxq(z, 0, "e4m3")
    x_two = unpack_weight(x_words, x_scales)[:, unstriped(two)]
    d = mxq(f64(w3), 0, "e4m3").T @ x_two
    return h + (sigmoid(d[np.arange(N)[:, None], runs(n4, N)] - d)) * (h[np.arange(N)[:, None], runs(n3, N)] - h)

@@ -1,0 +1,236 @@
+from contextlib import ExitStack
+
+import concourse.mybir as mybir
+
+F32 = mybir.dt.float32
+BF16 = mybir.dt.bfloat16
+I32 = mybir.dt.int32
+U32 = mybir.dt.uint32
+U16 = mybir.dt.uint16
+U8 = mybir.dt.uint8
+FP8X4 = mybir.dt.float8_e4m3fn_x4
+ALU = mybir.AluOpType
+ACT = mybir.ActivationFunctionType
+
+P = 128
+PACK = 4
+K, T, S = 512, 2048, 512
+HALF = S // 2
+LIST_COLS = S // 16
+SCALAR_SHARE = 24
+FLOPS = 3 * 2 * 512 * 512 * 512
+
+
+def tile_picked_latepullbhopp_none_p_kernel(
+    tc, x_words, x_scales, w1, gn, w2, w3, offs, n1, n2, two, n3, n4, out
+):
+    nc = tc.nc
+    with ExitStack() as ctx:
+        lists = ctx.enter_context(tc.tile_pool(name="lists", bufs=1))
+        keep = ctx.enter_context(tc.tile_pool(name="keep", bufs=1))
+        reuse = ctx.enter_context(tc.tile_pool(name="reuse", bufs=1))
+        early = ctx.enter_context(tc.tile_pool(name="early", bufs=1))
+        psum = ctx.enter_context(tc.psum_pool(name="psum", bufs=1))
+
+        def load_list(src, name):
+            dst = lists.tile([P, LIST_COLS], U16, name=name)
+            nc.sync.dma_start(dst[:], src)
+            return dst
+
+        def load_weight(w, c0, c1, name):
+            raw = keep.tile([P, PACK, c1 - c0], F32, name=name)
+            nc.sync.dma_start(raw[:], w.rearrange("(p j) c -> p j c", j=PACK)[:, :, c0:c1])
+            return raw
+
+        def dealt(grouped, raw, c0, c1):
+            dst = grouped[:].rearrange("p (t m j) -> p m j t", t=PACK, j=PACK)[:, c0 // PACK : c1 // PACK, :, :]
+            return dst, raw[:].rearrange("p j (m t) -> p m j t", t=PACK)
+
+        def chained_windows(name):
+            wins = [keep.tile([P, 2 * S], F32, name=f"{name}_win{t}") for t in range(PACK)]
+            last = keep.tile([P, S], F32, name=f"{name}_last")
+            nc.gpsimd.memset(wins[0][:, S:], 0.0)
+            return wins, [wins[t + 1][:, S:] for t in range(PACK - 1)] + [last[:]]
+
+        table_words = keep.tile([P, T], U32, name="table_words")
+        table_bytes = keep.tile([P, T], U8, name="table_bytes")
+        nc.gpsimd.memset(table_bytes[:].bitcast(I32), 0)
+        gain = keep.tile([P, PACK], F32, name="gain")
+        nc.scalar.dma_start(gain[:], gn.rearrange("(p t) o -> p (t o)", t=PACK))
+        is_zero = keep.tile([P, PACK], F32, name="is_zero")
+        safe_gain = keep.tile([P, PACK], F32, name="safe_gain")
+        inv_gain = keep.tile([P, PACK], F32, name="inv_gain")
+        nc.vector.tensor_scalar(is_zero[:], gain[:], 0.0, None, ALU.is_equal)
+        nc.vector.tensor_tensor(safe_gain[:], gain[:], is_zero[:], ALU.add)
+        nc.vector.reciprocal(inv_gain[:], safe_gain[:])
+        offs_t = load_list(offs, "offs_t")
+        nc.sync.dma_start(table_words[:].bitcast(I32), x_words[0].rearrange("p n r -> p (n r)").bitcast(I32))
+        for q in range(4):
+            nc.sync.dma_start(
+                table_bytes[:].bitcast(I32)[32 * q : 32 * q + 4, :], x_scales[0].bitcast(I32)[4 * q : 4 * q + 4, :]
+            )
+        w1_raw = [load_weight(w1, HALF * a, HALF * (a + 1), f"w1_raw{a}") for a in range(2)]
+        two_t = load_list(two, "two_t")
+        w3_raw = [load_weight(w3, HALF * a, HALF * (a + 1), f"w3_raw{a}") for a in range(2)]
+        n1_t = load_list(n1, "n1_t")
+        n2_t = load_list(n2, "n2_t")
+        w2_raw = load_weight(w2, 0, S, "w2_raw")
+        n4_t = load_list(n4, "n4_t")
+        n3_t = load_list(n3, "n3_t")
+
+        y_win, y_own = chained_windows("y")
+        d_win, d_own = chained_windows("d")
+        h_win, h_own = chained_windows("h")
+
+        x1_words = keep.tile([P, S], U32, name="x1_words", align_bytes=64)
+        x1_bytes = keep.tile([P, S], U8, name="x1_bytes", align_bytes=64)
+        nc.vector.tensor_copy(x1_words[:], table_words[:].indirect(offs_t[:]))
+        nc.vector.tensor_copy(x1_bytes[:], table_bytes[:].indirect(offs_t[:]))
+
+        w1_grouped = early.tile([P, PACK * S], BF16, name="w1_grouped", align_bytes=64, offset=0)
+        dst, src = dealt(w1_grouped, w1_raw[0], 0, HALF)
+        nc.scalar.activation(dst, src, ACT.Copy)
+        dst, src = dealt(w1_grouped, w1_raw[1], HALF, S)
+        nc.scalar.activation(dst[:, :SCALAR_SHARE], src[:, :SCALAR_SHARE], ACT.Copy)
+        nc.vector.tensor_copy(dst[:, SCALAR_SHARE:], src[:, SCALAR_SHARE:])
+
+        def product(bank, codes, scales, t, words, scale_bytes):
+            cols = slice(P * t, P * (t + 1))
+            nc.tensor.matmul_mx(
+                out=bank,
+                lhsT=codes[:, cols].bitcast(FP8X4),
+                lhsT_scale=scales[:, cols],
+                rhs=words.bitcast(FP8X4),
+                rhs_scale=scale_bytes,
+                start=True,
+                stop=True,
+            )
+
+        w1_codes = keep.tile([P, S], U32, name="w1_codes", align_bytes=64)
+        w1_scales = keep.tile([P, S], U8, name="w1_scales", align_bytes=64)
+        y_bank = [psum.tile([P, S], F32, name=f"y_bank{t}", tag=f"yh{t}") for t in range(PACK)]
+        for t0, t1 in ((0, 1), (1, 2), (2, 4)):
+            cols = slice(P * t0, P * t1)
+            nc.vector.quantize_mx(
+                out=w1_codes[:, cols].bitcast(FP8X4), scales=w1_scales[:, cols], in_=w1_grouped[:, S * t0 : S * t1]
+            )
+            for t in range(t0, t1):
+                product(y_bank[t][:], w1_codes, w1_scales, t, x1_words[:], x1_bytes[:])
+
+        x2_words = early.tile([P, S], U32, name="x2_words", align_bytes=64, offset=0)
+        x2_bytes = early.tile([P, S], U8, name="x2_bytes", align_bytes=64, offset=4 * S)
+        nc.vector.tensor_copy(x2_words[:], table_words[:].indirect(two_t[:]))
+        nc.vector.tensor_copy(x2_bytes[:], table_bytes[:].indirect(two_t[:]))
+
+        for t in range(PACK):
+            nc.scalar.activation(y_win[t][:, :S], y_bank[t][:], ACT.Copy, scale=gain[:, t : t + 1])
+            nc.scalar.activation(y_own[t], y_bank[t][:], ACT.Copy, scale=gain[:, t : t + 1])
+
+        st_gain = [keep.tile([P, S], F32, name=f"st_gain{t}") for t in range(PACK)]
+        st_tanh = [reuse.tile([P, S], F32, name=f"st_tanh{t}", align_bytes=64) for t in range(PACK)]
+        for t in range(PACK):
+            nc.vector.tensor_tensor(st_gain[t][:], y_win[t][:].indirect(n1_t[:]), y_own[t], ALU.add)
+        for t in range(PACK):
+            nc.scalar.activation(st_tanh[t][:], st_gain[t][:], ACT.Tanh, scale=inv_gain[:, t : t + 1])
+
+        w3_grouped = reuse.tile([P, PACK * S], BF16, name="w3_grouped", tag="w3_then_z", align_bytes=64)
+        for a in range(2):
+            dst, src = dealt(w3_grouped, w3_raw[a], HALF * a, HALF * (a + 1))
+            nc.scalar.activation(dst, src, ACT.Copy)
+
+        halves = [slice(0, HALF), slice(HALF, S)]
+        z_planes = [keep.tile([P, PACK, HALF], F32, name="z_planes0")]
+        z_grouped = [keep.tile([P, HALF, PACK], BF16, name=f"z_grouped{a}", align_bytes=64) for a in range(2)]
+        z_codes = [keep.tile([P, HALF], U32, name=f"z_codes{a}", align_bytes=64) for a in range(2)]
+        z_scales = [keep.tile([P, HALF], U8, name=f"z_scales{a}", align_bytes=64) for a in range(2)]
+
+        def gather_z(a):
+            for t in range(PACK):
+                nc.vector.tensor_tensor(
+                    z_planes[a][:, t, :],
+                    st_tanh[t][:].indirect(n2_t[:, LIST_COLS // 2 * a : LIST_COLS // 2 * (a + 1)]),
+                    st_gain[t][:, halves[a]],
+                    ALU.mult,
+                )
+
+        def group_z(a):
+            nc.scalar.activation(
+                z_grouped[a][:].rearrange("p (c i) t -> p c t i", i=4),
+                z_planes[a][:].rearrange("p t (c i) -> p c t i", i=4),
+                ACT.Copy,
+            )
+
+        def quantise_z(a):
+            nc.vector.quantize_mx(
+                out=z_codes[a][:].bitcast(FP8X4),
+                scales=z_scales[a][:],
+                in_=z_grouped[a][:].rearrange("p c t -> p (c t)"),
+            )
+
+        def leave_bank(bank, win, own):
+            nc.scalar.copy(win[:, :S], bank[:])
+            nc.scalar.copy(own, bank[:])
+
+        w3_codes = keep.tile([P, S], U32, name="w3_codes", align_bytes=64)
+        w3_scales = keep.tile([P, S], U8, name="w3_scales", align_bytes=64)
+        w2_codes = keep.tile([P, S], U32, name="w2_codes", align_bytes=64)
+        w2_scales = keep.tile([P, S], U8, name="w2_scales", align_bytes=64)
+        d_bank = [psum.tile([P, S], F32, name=f"d_bank{t}") for t in range(PACK)]
+        h_bank = [psum.tile([P, S], F32, name=f"h_bank{t}", tag=f"yh{t}") for t in range(PACK)]
+
+        gather_z(0)
+        nc.vector.quantize_mx(out=w3_codes[:].bitcast(FP8X4), scales=w3_scales[:], in_=w3_grouped[:])
+        for t in range(PACK):
+            product(d_bank[t][:], w3_codes, w3_scales, t, x2_words[:], x2_bytes[:])
+        group_z(0)
+        leave_bank(d_bank[0], d_win[0], d_own[0])
+        z_planes.append(reuse.tile([P, PACK, HALF], F32, name="z_planes1", tag="w3_then_z", align_bytes=64))
+        gather_z(1)
+        group_z(1)
+        w2_grouped = reuse.tile([P, PACK * S], BF16, name="w2_grouped", tag=f"st_tanh{PACK - 1}", align_bytes=64)
+        dst, src = dealt(w2_grouped, w2_raw, 0, S)
+        nc.vector.tensor_copy(dst, src)
+        quantise_z(0)
+        nc.vector.quantize_mx(out=w2_codes[:].bitcast(FP8X4), scales=w2_scales[:], in_=w2_grouped[:])
+        quantise_z(1)
+        for t in range(PACK):
+            for a in range(2):
+                product(h_bank[t][:, halves[a]], w2_codes, w2_scales, t, z_codes[a][:], z_scales[a][:])
+
+        out_rows = out.rearrange("(p t) j -> p t j", t=PACK)
+        d_step = [keep.tile([P, S], F32, name=f"d_step{t}") for t in range(PACK)]
+        gate = [keep.tile([P, S], F32, name=f"gate{t}") for t in range(PACK)]
+        h_step = [keep.tile([P, S], F32, name=f"h_step{t}") for t in range(PACK)]
+        pull = [keep.tile([P, S], F32, name=f"pull{t}") for t in range(PACK)]
+        result = [keep.tile([P, S], F32, name=f"result{t}") for t in range(PACK)]
+
+        def gather_d(t):
+            nc.vector.tensor_tensor(d_step[t][:], d_win[t][:].indirect(n4_t[:]), d_own[t], ALU.subtract)
+
+        def gather_h(t):
+            nc.vector.tensor_tensor(h_step[t][:], h_win[t][:].indirect(n3_t[:]), h_own[t], ALU.subtract)
+
+        def pull_of(t, cols):
+            nc.vector.scalar_tensor_tensor(pull[t][:, cols], gate[t][:, cols], 1.0, h_step[t][:, cols], ALU.add, ALU.mult)
+
+        def result_of(t, cols):
+            nc.vector.scalar_tensor_tensor(result[t][:, cols], pull[t][:, cols], 0.5, h_own[t][:, cols], ALU.mult, ALU.add)
+            nc.sync.dma_start(out_rows[:, t, cols], result[t][:, cols])
+
+        whole = slice(0, S)
+        gather_d(0)
+        for t in range(PACK):
+            if t + 1 < PACK:
+                leave_bank(d_bank[t + 1], d_win[t + 1], d_own[t + 1])
+                gather_d(t + 1)
+            if t > 0:
+                pull_of(t - 1, whole)
+            leave_bank(h_bank[t], h_win[t], h_own[t])
+            nc.scalar.activation(gate[t][:], d_step[t][:], ACT.Tanh, scale=0.5)
+            gather_h(t)
+            if t > 0:
+                result_of(t - 1, whole)
+        for cols in halves:
+            pull_of(PACK - 1, cols)
+        for cols in halves:
+            result_of(PACK - 1, cols)

@@ -47,9 +47,8 @@ def tile_picked_latepullbhopp_none_p_kernel(
             return dst, raw[:].rearrange("p j (m t) -> p m j t", t=PACK)
 
         def chained_windows(name):
-            wins = [keep.tile([P, 2 * S], F32, name=f"{name}_win{t}") for t in range(PACK)]
+            wins = [reuse.tile([P, 2 * S], F32, name=f"{name}_win{t}", align_bytes=64) for t in range(PACK)]
             last = keep.tile([P, S], F32, name=f"{name}_last")
-            nc.gpsimd.memset(wins[0][:, S:], 0.0)
             return wins, [wins[t + 1][:, S:] for t in range(PACK - 1)] + [last[:]]
 
         table_words = keep.tile([P, T], U32, name="table_words")
@@ -71,16 +70,20 @@ def tile_picked_latepullbhopp_none_p_kernel(
             )
         w1_raw = [load_weight(w1, HALF * a, HALF * (a + 1), f"w1_raw{a}") for a in range(2)]
         two_t = load_list(two, "two_t")
-        w3_raw = [load_weight(w3, HALF * a, HALF * (a + 1), f"w3_raw{a}") for a in range(2)]
+        w3_raw = [load_weight(w3, 0, HALF, "w3_raw0")]
         n1_t = load_list(n1, "n1_t")
         n2_t = load_list(n2, "n2_t")
         w2_raw = load_weight(w2, 0, S, "w2_raw")
+        w3_raw.append(load_weight(w3, HALF, S, "w3_raw1"))
         n4_t = load_list(n4, "n4_t")
         n3_t = load_list(n3, "n3_t")
 
         y_win, y_own = chained_windows("y")
         d_win, d_own = chained_windows("d")
         h_win, h_own = chained_windows("h")
+        nc.scalar.activation(y_win[0][:, S:], gain[:, 0:1].to_broadcast([P, S]), ACT.Sigmoid)
+        nc.gpsimd.memset(d_win[0][:, S:], 0.0)
+        nc.gpsimd.memset(h_win[0][:, S:], 0.0)
 
         x1_words = keep.tile([P, S], U32, name="x1_words", align_bytes=64)
         x1_bytes = keep.tile([P, S], U8, name="x1_bytes", align_bytes=64)
@@ -182,14 +185,16 @@ def tile_picked_latepullbhopp_none_p_kernel(
         nc.vector.quantize_mx(out=w3_codes[:].bitcast(FP8X4), scales=w3_scales[:], in_=w3_grouped[:])
         for t in range(PACK):
             product(d_bank[t][:], w3_codes, w3_scales, t, x2_words[:], x2_bytes[:])
+        w2_grouped = reuse.tile([P, PACK * S], BF16, name="w2_grouped", tag="y_win0", align_bytes=64)
+        w2_dst, w2_src = dealt(w2_grouped, w2_raw, 0, S)
+        nc.scalar.activation(w2_dst[:, : P // 2], w2_src[:, : P // 2], ACT.Copy)
         group_z(0)
-        leave_bank(d_bank[0], d_win[0], d_own[0])
+        nc.scalar.activation(w2_dst[:, P // 2 :], w2_src[:, P // 2 :], ACT.Copy)
+        nc.scalar.copy(d_win[0][:, :S], d_bank[0][:])
         z_planes.append(reuse.tile([P, PACK, HALF], F32, name="z_planes1", tag="w3_then_z", align_bytes=64))
         gather_z(1)
         group_z(1)
-        w2_grouped = reuse.tile([P, PACK * S], BF16, name="w2_grouped", tag=f"st_tanh{PACK - 1}", align_bytes=64)
-        dst, src = dealt(w2_grouped, w2_raw, 0, S)
-        nc.vector.tensor_copy(dst, src)
+        nc.scalar.copy(d_own[0], d_bank[0][:])
         quantise_z(0)
         nc.vector.quantize_mx(out=w2_codes[:].bitcast(FP8X4), scales=w2_scales[:], in_=w2_grouped[:])
         quantise_z(1)
@@ -198,39 +203,24 @@ def tile_picked_latepullbhopp_none_p_kernel(
                 product(h_bank[t][:, halves[a]], w2_codes, w2_scales, t, z_codes[a][:], z_scales[a][:])
 
         out_rows = out.rearrange("(p t) j -> p t j", t=PACK)
-        d_step = [keep.tile([P, S], F32, name=f"d_step{t}") for t in range(PACK)]
-        gate = [keep.tile([P, S], F32, name=f"gate{t}") for t in range(PACK)]
-        h_step = [keep.tile([P, S], F32, name=f"h_step{t}") for t in range(PACK)]
-        pull = [keep.tile([P, S], F32, name=f"pull{t}") for t in range(PACK)]
-        result = [keep.tile([P, S], F32, name=f"result{t}") for t in range(PACK)]
-
-        def gather_d(t):
-            nc.vector.tensor_tensor(d_step[t][:], d_win[t][:].indirect(n4_t[:]), d_own[t], ALU.subtract)
-
-        def gather_h(t):
-            nc.vector.tensor_tensor(h_step[t][:], h_win[t][:].indirect(n3_t[:]), h_own[t], ALU.subtract)
-
-        def pull_of(t, cols):
-            nc.vector.scalar_tensor_tensor(pull[t][:, cols], gate[t][:, cols], 1.0, h_step[t][:, cols], ALU.add, ALU.mult)
-
-        def result_of(t, cols):
-            nc.vector.scalar_tensor_tensor(result[t][:, cols], pull[t][:, cols], 0.5, h_own[t][:, cols], ALU.mult, ALU.add)
-            nc.sync.dma_start(out_rows[:, t, cols], result[t][:, cols])
-
-        whole = slice(0, S)
-        gather_d(0)
-        for t in range(PACK):
-            if t + 1 < PACK:
-                leave_bank(d_bank[t + 1], d_win[t + 1], d_own[t + 1])
-                gather_d(t + 1)
-            if t > 0:
-                pull_of(t - 1, whole)
-            leave_bank(h_bank[t], h_win[t], h_own[t])
-            nc.scalar.activation(gate[t][:], d_step[t][:], ACT.Tanh, scale=0.5)
-            gather_h(t)
-            if t > 0:
-                result_of(t - 1, whole)
-        for cols in halves:
-            pull_of(PACK - 1, cols)
-        for cols in halves:
-            result_of(PACK - 1, cols)
+        for pair in range(PACK // 2):
+            tiles = (2 * pair, 2 * pair + 1)
+            d_step = keep.tile([P, 2, S], F32, name=f"d_step{pair}")
+            gate = keep.tile([P, 2, S], F32, name=f"gate{pair}")
+            h_step = keep.tile([P, 2, S], F32, name=f"h_step{pair}")
+            pull = keep.tile([P, 2, S], F32, name=f"pull{pair}")
+            result = keep.tile([P, 2, S], F32, name=f"result{pair}")
+            for i, t in enumerate(tiles):
+                if t > 0:
+                    leave_bank(d_bank[t], d_win[t], d_own[t])
+                nc.vector.tensor_tensor(d_step[:, i, :], d_win[t][:].indirect(n4_t[:]), d_own[t], ALU.subtract)
+            for i, t in enumerate(tiles):
+                leave_bank(h_bank[t], h_win[t], h_own[t])
+                nc.vector.tensor_tensor(h_step[:, i, :], h_win[t][:].indirect(n3_t[:]), h_own[t], ALU.subtract)
+            nc.scalar.activation(gate[:], d_step[:], ACT.Sigmoid)
+            for i, t in enumerate(tiles):
+                nc.vector.tensor_tensor(pull[:, i, :], gate[:, i, :], h_step[:, i, :], ALU.mult)
+            for i, t in enumerate(tiles):
+                for cols in halves if t == PACK - 1 else [slice(0, S)]:
+                    nc.vector.tensor_tensor(result[:, i, cols], pull[:, i, cols], h_own[t][:, cols], ALU.add)
+                    nc.sync.dma_start(out_rows[:, t, cols], result[:, i, cols])

@@ -17,7 +17,6 @@ PACK = 4
 K, T, S = 512, 2048, 512
 HALF = S // 2
 LIST_COLS = S // 16
-SCALAR_SHARE = 24
 FLOPS = 3 * 2 * 512 * 512 * 512
 
 
@@ -29,7 +28,6 @@ def tile_picked_latepullbhopp_none_p_kernel(
         lists = ctx.enter_context(tc.tile_pool(name="lists", bufs=1))
         keep = ctx.enter_context(tc.tile_pool(name="keep", bufs=1))
         reuse = ctx.enter_context(tc.tile_pool(name="reuse", bufs=1))
-        early = ctx.enter_context(tc.tile_pool(name="early", bufs=1))
         psum = ctx.enter_context(tc.psum_pool(name="psum", bufs=1))
 
         def load_list(src, name):
@@ -79,9 +77,11 @@ def tile_picked_latepullbhopp_none_p_kernel(
         n3_t = load_list(n3, "n3_t")
 
         y_win, y_own = chained_windows("y")
+        tanh_win, st_gain = chained_windows("tanh")
         d_win, d_own = chained_windows("d")
         h_win, h_own = chained_windows("h")
         nc.scalar.activation(y_win[0][:, S:], gain[:, 0:1].to_broadcast([P, S]), ACT.Sigmoid)
+        nc.gpsimd.memset(tanh_win[0][:, S:], 0.0)
         nc.gpsimd.memset(d_win[0][:, S:], 0.0)
         nc.gpsimd.memset(h_win[0][:, S:], 0.0)
 
@@ -90,12 +90,12 @@ def tile_picked_latepullbhopp_none_p_kernel(
         nc.vector.tensor_copy(x1_words[:], table_words[:].indirect(offs_t[:]))
         nc.vector.tensor_copy(x1_bytes[:], table_bytes[:].indirect(offs_t[:]))
 
-        w1_grouped = early.tile([P, PACK * S], BF16, name="w1_grouped", align_bytes=64, offset=0)
-        dst, src = dealt(w1_grouped, w1_raw[0], 0, HALF)
-        nc.scalar.activation(dst, src, ACT.Copy)
-        dst, src = dealt(w1_grouped, w1_raw[1], HALF, S)
-        nc.scalar.activation(dst[:, :SCALAR_SHARE], src[:, :SCALAR_SHARE], ACT.Copy)
-        nc.vector.tensor_copy(dst[:, SCALAR_SHARE:], src[:, SCALAR_SHARE:])
+        w1_grouped = reuse.tile([P, PACK * S], BF16, name="w1_grouped", align_bytes=64)
+        for a in range(2):
+            dst, src = dealt(w1_grouped, w1_raw[a], HALF * a, HALF * (a + 1))
+            nc.scalar.activation(dst, src, ACT.Copy)
+        x2_words = keep.tile([P, S], U32, name="x2_words", align_bytes=64)
+        nc.vector.tensor_copy(x2_words[:], table_words[:].indirect(two_t[:]))
 
         def product(bank, codes, scales, t, words, scale_bytes):
             cols = slice(P * t, P * (t + 1))
@@ -120,104 +120,78 @@ def tile_picked_latepullbhopp_none_p_kernel(
             for t in range(t0, t1):
                 product(y_bank[t][:], w1_codes, w1_scales, t, x1_words[:], x1_bytes[:])
 
-        x2_words = early.tile([P, S], U32, name="x2_words", align_bytes=64, offset=0)
-        x2_bytes = early.tile([P, S], U8, name="x2_bytes", align_bytes=64, offset=4 * S)
-        nc.vector.tensor_copy(x2_words[:], table_words[:].indirect(two_t[:]))
+        x2_bytes = reuse.tile([P, S], U8, name="x2_bytes", tag="w1_grouped", align_bytes=64)
         nc.vector.tensor_copy(x2_bytes[:], table_bytes[:].indirect(two_t[:]))
 
         for t in range(PACK):
             nc.scalar.activation(y_win[t][:, :S], y_bank[t][:], ACT.Copy, scale=gain[:, t : t + 1])
             nc.scalar.activation(y_own[t], y_bank[t][:], ACT.Copy, scale=gain[:, t : t + 1])
 
-        st_gain = [keep.tile([P, S], F32, name=f"st_gain{t}") for t in range(PACK)]
-        st_tanh = [reuse.tile([P, S], F32, name=f"st_tanh{t}", align_bytes=64) for t in range(PACK)]
         for t in range(PACK):
-            nc.vector.tensor_tensor(st_gain[t][:], y_win[t][:].indirect(n1_t[:]), y_own[t], ALU.add)
-        for t in range(PACK):
-            nc.scalar.activation(st_tanh[t][:], st_gain[t][:], ACT.Tanh, scale=inv_gain[:, t : t + 1])
+            nc.vector.tensor_tensor(st_gain[t], y_win[t][:].indirect(n1_t[:]), y_own[t], ALU.add)
 
-        w3_grouped = reuse.tile([P, PACK * S], BF16, name="w3_grouped", tag="w3_then_z", align_bytes=64)
-        for a in range(2):
-            dst, src = dealt(w3_grouped, w3_raw[a], HALF * a, HALF * (a + 1))
-            nc.scalar.activation(dst, src, ACT.Copy)
+        def deal_halves(grouped, raws):
+            for a in range(2):
+                dst, src = dealt(grouped, raws[a], HALF * a, HALF * (a + 1))
+                nc.scalar.activation(dst, src, ACT.Copy)
 
-        halves = [slice(0, HALF), slice(HALF, S)]
-        z_planes = [keep.tile([P, PACK, HALF], F32, name="z_planes0")]
-        z_grouped = [keep.tile([P, HALF, PACK], BF16, name=f"z_grouped{a}", align_bytes=64) for a in range(2)]
-        z_codes = [keep.tile([P, HALF], U32, name=f"z_codes{a}", align_bytes=64) for a in range(2)]
-        z_scales = [keep.tile([P, HALF], U8, name=f"z_scales{a}", align_bytes=64) for a in range(2)]
+        def quantise(grouped, name):
+            codes = reuse.tile([P, S], U32, name=f"{name}_codes", align_bytes=64)
+            scales = reuse.tile([P, S], U8, name=f"{name}_scales", align_bytes=64)
+            nc.vector.quantize_mx(out=codes[:].bitcast(FP8X4), scales=scales[:], in_=grouped[:])
+            return codes, scales
 
-        def gather_z(a):
-            for t in range(PACK):
-                nc.vector.tensor_tensor(
-                    z_planes[a][:, t, :],
-                    st_tanh[t][:].indirect(n2_t[:, LIST_COLS // 2 * a : LIST_COLS // 2 * (a + 1)]),
-                    st_gain[t][:, halves[a]],
-                    ALU.mult,
-                )
-
-        def group_z(a):
-            nc.scalar.activation(
-                z_grouped[a][:].rearrange("p (c i) t -> p c t i", i=4),
-                z_planes[a][:].rearrange("p t (c i) -> p c t i", i=4),
-                ACT.Copy,
-            )
-
-        def quantise_z(a):
-            nc.vector.quantize_mx(
-                out=z_codes[a][:].bitcast(FP8X4),
-                scales=z_scales[a][:],
-                in_=z_grouped[a][:].rearrange("p c t -> p (c t)"),
-            )
-
-        def leave_bank(bank, win, own):
-            nc.scalar.copy(win[:, :S], bank[:])
-            nc.scalar.copy(own, bank[:])
-
-        w3_codes = keep.tile([P, S], U32, name="w3_codes", align_bytes=64)
-        w3_scales = keep.tile([P, S], U8, name="w3_scales", align_bytes=64)
-        w2_codes = keep.tile([P, S], U32, name="w2_codes", align_bytes=64)
-        w2_scales = keep.tile([P, S], U8, name="w2_scales", align_bytes=64)
+        w3_grouped = keep.tile([P, PACK * S], BF16, name="w3_grouped", align_bytes=64)
+        deal_halves(w3_grouped, w3_raw)
+        w3_codes, w3_scales = quantise(w3_grouped, "w3")
         d_bank = [psum.tile([P, S], F32, name=f"d_bank{t}") for t in range(PACK)]
-        h_bank = [psum.tile([P, S], F32, name=f"h_bank{t}", tag=f"yh{t}") for t in range(PACK)]
-
-        gather_z(0)
-        nc.vector.quantize_mx(out=w3_codes[:].bitcast(FP8X4), scales=w3_scales[:], in_=w3_grouped[:])
         for t in range(PACK):
             product(d_bank[t][:], w3_codes, w3_scales, t, x2_words[:], x2_bytes[:])
+
+        z_planes = keep.tile([P, PACK, S], F32, name="z_planes")
+        for t in range(PACK):
+            nc.scalar.activation(tanh_win[t][:, :S], st_gain[t], ACT.Tanh, scale=inv_gain[:, t : t + 1])
+            nc.vector.tensor_tensor(z_planes[:, t, :], tanh_win[t][:].indirect(n2_t[:]), st_gain[t], ALU.mult)
+
+        for t in range(PACK):
+            nc.scalar.copy(d_win[t][:, :S], d_bank[t][:])
+            nc.sync.dma_start(d_own[t], d_win[t][:, :S])
+
         w2_grouped = reuse.tile([P, PACK * S], BF16, name="w2_grouped", tag="y_win0", align_bytes=64)
         w2_dst, w2_src = dealt(w2_grouped, w2_raw, 0, S)
-        nc.scalar.activation(w2_dst[:, : P // 2], w2_src[:, : P // 2], ACT.Copy)
-        group_z(0)
-        nc.scalar.activation(w2_dst[:, P // 2 :], w2_src[:, P // 2 :], ACT.Copy)
-        nc.scalar.copy(d_win[0][:, :S], d_bank[0][:])
-        z_planes.append(reuse.tile([P, PACK, HALF], F32, name="z_planes1", tag="w3_then_z", align_bytes=64))
-        gather_z(1)
-        group_z(1)
-        nc.scalar.copy(d_own[0], d_bank[0][:])
-        quantise_z(0)
-        nc.vector.quantize_mx(out=w2_codes[:].bitcast(FP8X4), scales=w2_scales[:], in_=w2_grouped[:])
-        quantise_z(1)
+        nc.scalar.activation(w2_dst, w2_src, ACT.Copy)
+        z_grouped = reuse.tile([P, PACK * S], BF16, name="z_grouped", align_bytes=64)
+        nc.scalar.activation(
+            z_grouped[:].rearrange("p (c i t) -> p c t i", i=4, t=PACK),
+            z_planes[:].rearrange("p t (c i) -> p c t i", i=4),
+            ACT.Copy,
+        )
+        w2_codes, w2_scales = quantise(w2_grouped, "w2")
+        z_codes, z_scales = quantise(z_grouped, "z")
+        h_bank = [psum.tile([P, S], F32, name=f"h_bank{t}", tag=f"yh{t}") for t in range(PACK)]
         for t in range(PACK):
-            for a in range(2):
-                product(h_bank[t][:, halves[a]], w2_codes, w2_scales, t, z_codes[a][:], z_scales[a][:])
+            product(h_bank[t][:], w2_codes, w2_scales, t, z_codes[:], z_scales[:])
+
+        d_step = [
+            keep.tile([P, 2, S], F32, name="d_step0"),
+            reuse.tile([P, 2, S], F32, name="d_step1", tag="z_grouped", align_bytes=64),
+        ]
+        for t in range(PACK):
+            nc.vector.tensor_tensor(d_step[t // 2][:, t % 2, :], d_win[t][:].indirect(n4_t[:]), d_own[t], ALU.subtract)
 
         out_rows = out.rearrange("(p t) j -> p t j", t=PACK)
-        for pair in range(PACK // 2):
+        halves = [slice(0, HALF), slice(HALF, S)]
+        for pair, spent in enumerate(("z_codes", "w2_codes")):
             tiles = (2 * pair, 2 * pair + 1)
-            d_step = keep.tile([P, 2, S], F32, name=f"d_step{pair}")
-            gate = keep.tile([P, 2, S], F32, name=f"gate{pair}")
+            gate = reuse.tile([P, 2, S], F32, name=f"gate{pair}", tag=spent, align_bytes=64)
             h_step = keep.tile([P, 2, S], F32, name=f"h_step{pair}")
             pull = keep.tile([P, 2, S], F32, name=f"pull{pair}")
             result = keep.tile([P, 2, S], F32, name=f"result{pair}")
             for i, t in enumerate(tiles):
-                if t > 0:
-                    leave_bank(d_bank[t], d_win[t], d_own[t])
-                nc.vector.tensor_tensor(d_step[:, i, :], d_win[t][:].indirect(n4_t[:]), d_own[t], ALU.subtract)
-            for i, t in enumerate(tiles):
-                leave_bank(h_bank[t], h_win[t], h_own[t])
+                nc.scalar.copy(h_win[t][:, :S], h_bank[t][:])
+                nc.scalar.copy(h_own[t], h_bank[t][:])
                 nc.vector.tensor_tensor(h_step[:, i, :], h_win[t][:].indirect(n3_t[:]), h_own[t], ALU.subtract)
-            nc.scalar.activation(gate[:], d_step[:], ACT.Sigmoid)
+            nc.scalar.activation(gate[:], d_step[pair][:], ACT.Sigmoid)
             for i, t in enumerate(tiles):
                 nc.vector.tensor_tensor(pull[:, i, :], gate[:, i, :], h_step[:, i, :], ALU.mult)
             for i, t in enumerate(tiles):

@@ -36,7 +36,7 @@ def tile_picked_latepullbhopp_none_p_kernel(
             return dst
 
         def load_weight(w, c0, c1, name):
-            raw = keep.tile([P, PACK, c1 - c0], F32, name=name)
+            raw = reuse.tile([P, PACK, c1 - c0], F32, name=name, align_bytes=64)
             nc.sync.dma_start(raw[:], w.rearrange("(p j) c -> p j c", j=PACK)[:, :, c0:c1])
             return raw
 
@@ -62,12 +62,12 @@ def tile_picked_latepullbhopp_none_p_kernel(
         nc.vector.reciprocal(inv_gain[:], safe_gain[:])
         offs_t = load_list(offs, "offs_t")
         nc.sync.dma_start(table_words[:].bitcast(I32), x_words[0].rearrange("p n r -> p (n r)").bitcast(I32))
+        two_t = load_list(two, "two_t")
         for q in range(4):
             nc.sync.dma_start(
                 table_bytes[:].bitcast(I32)[32 * q : 32 * q + 4, :], x_scales[0].bitcast(I32)[4 * q : 4 * q + 4, :]
             )
         w1_raw = [load_weight(w1, HALF * a, HALF * (a + 1), f"w1_raw{a}") for a in range(2)]
-        two_t = load_list(two, "two_t")
         w3_raw = [load_weight(w3, 0, HALF, "w3_raw0")]
         n1_t = load_list(n1, "n1_t")
         n2_t = load_list(n2, "n2_t")
@@ -88,14 +88,14 @@ def tile_picked_latepullbhopp_none_p_kernel(
         x1_words = keep.tile([P, S], U32, name="x1_words", align_bytes=64)
         x1_bytes = keep.tile([P, S], U8, name="x1_bytes", align_bytes=64)
         nc.vector.tensor_copy(x1_words[:], table_words[:].indirect(offs_t[:]))
+        x2_words = keep.tile([P, S], U32, name="x2_words", align_bytes=64)
+        nc.vector.tensor_copy(x2_words[:], table_words[:].indirect(two_t[:]))
         nc.vector.tensor_copy(x1_bytes[:], table_bytes[:].indirect(offs_t[:]))
 
-        w1_grouped = reuse.tile([P, PACK * S], BF16, name="w1_grouped", align_bytes=64)
+        w1_grouped = keep.tile([P, PACK * S], BF16, name="w1_grouped", align_bytes=64)
         for a in range(2):
             dst, src = dealt(w1_grouped, w1_raw[a], HALF * a, HALF * (a + 1))
             nc.scalar.activation(dst, src, ACT.Copy)
-        x2_words = keep.tile([P, S], U32, name="x2_words", align_bytes=64)
-        nc.vector.tensor_copy(x2_words[:], table_words[:].indirect(two_t[:]))
 
         def product(bank, codes, scales, t, words, scale_bytes):
             cols = slice(P * t, P * (t + 1))
@@ -112,20 +112,25 @@ def tile_picked_latepullbhopp_none_p_kernel(
         w1_codes = keep.tile([P, S], U32, name="w1_codes", align_bytes=64)
         w1_scales = keep.tile([P, S], U8, name="w1_scales", align_bytes=64)
         y_bank = [psum.tile([P, S], F32, name=f"y_bank{t}", tag=f"yh{t}") for t in range(PACK)]
+        y_spare = psum.tile([P, HALF], F32, name="y_spare", tag="d_bank3")
+        y_parts = [[(y_bank[0][:, :HALF], slice(0, HALF)), (y_spare[:], slice(HALF, S))]]
+        y_parts.extend([(y_bank[t][:], slice(0, S))] for t in range(1, PACK))
         for t0, t1 in ((0, 1), (1, 2), (2, 4)):
             cols = slice(P * t0, P * t1)
             nc.vector.quantize_mx(
                 out=w1_codes[:, cols].bitcast(FP8X4), scales=w1_scales[:, cols], in_=w1_grouped[:, S * t0 : S * t1]
             )
             for t in range(t0, t1):
-                product(y_bank[t][:], w1_codes, w1_scales, t, x1_words[:], x1_bytes[:])
+                for bank, cols in y_parts[t]:
+                    product(bank, w1_codes, w1_scales, t, x1_words[:, cols], x1_bytes[:, cols])
 
-        x2_bytes = reuse.tile([P, S], U8, name="x2_bytes", tag="w1_grouped", align_bytes=64)
+        x2_bytes = reuse.tile([P, S], U8, name="x2_bytes", tag="w1_raw1", align_bytes=64)
         nc.vector.tensor_copy(x2_bytes[:], table_bytes[:].indirect(two_t[:]))
 
         for t in range(PACK):
-            nc.scalar.activation(y_win[t][:, :S], y_bank[t][:], ACT.Copy, scale=gain[:, t : t + 1])
-            nc.scalar.activation(y_own[t], y_bank[t][:], ACT.Copy, scale=gain[:, t : t + 1])
+            for bank, cols in y_parts[t]:
+                nc.scalar.activation(y_win[t][:, cols], bank, ACT.Copy, scale=gain[:, t : t + 1])
+                nc.scalar.activation(y_own[t][:, cols], bank, ACT.Copy, scale=gain[:, t : t + 1])
 
         for t in range(PACK):
             nc.vector.tensor_tensor(st_gain[t], y_win[t][:].indirect(n1_t[:]), y_own[t], ALU.add)
@@ -148,24 +153,30 @@ def tile_picked_latepullbhopp_none_p_kernel(
         for t in range(PACK):
             product(d_bank[t][:], w3_codes, w3_scales, t, x2_words[:], x2_bytes[:])
 
-        z_planes = keep.tile([P, PACK, S], F32, name="z_planes")
+        z_planes = reuse.tile([P, PACK, S], F32, name="z_planes", align_bytes=64)
         for t in range(PACK):
             nc.scalar.activation(tanh_win[t][:, :S], st_gain[t], ACT.Tanh, scale=inv_gain[:, t : t + 1])
             nc.vector.tensor_tensor(z_planes[:, t, :], tanh_win[t][:].indirect(n2_t[:]), st_gain[t], ALU.mult)
 
-        for t in range(PACK):
+        def leave_by_dma(t):
             nc.scalar.copy(d_win[t][:, :S], d_bank[t][:])
             nc.sync.dma_start(d_own[t], d_win[t][:, :S])
+
+        leave_by_dma(0)
+        leave_by_dma(1)
 
         w2_grouped = reuse.tile([P, PACK * S], BF16, name="w2_grouped", tag="y_win0", align_bytes=64)
         w2_dst, w2_src = dealt(w2_grouped, w2_raw, 0, S)
         nc.scalar.activation(w2_dst, w2_src, ACT.Copy)
-        z_grouped = reuse.tile([P, PACK * S], BF16, name="z_grouped", align_bytes=64)
+        leave_by_dma(2)
+        z_grouped = keep.tile([P, PACK * S], BF16, name="z_grouped", align_bytes=64)
         nc.scalar.activation(
             z_grouped[:].rearrange("p (c i t) -> p c t i", i=4, t=PACK),
             z_planes[:].rearrange("p t (c i) -> p c t i", i=4),
             ACT.Copy,
         )
+        nc.scalar.copy(d_win[3][:, :S], d_bank[3][:])
+        nc.scalar.copy(d_own[3], d_bank[3][:])
         w2_codes, w2_scales = quantise(w2_grouped, "w2")
         z_codes, z_scales = quantise(z_grouped, "z")
         h_bank = [psum.tile([P, S], F32, name=f"h_bank{t}", tag=f"yh{t}") for t in range(PACK)]
@@ -174,13 +185,12 @@ def tile_picked_latepullbhopp_none_p_kernel(
 
         d_step = [
             keep.tile([P, 2, S], F32, name="d_step0"),
-            reuse.tile([P, 2, S], F32, name="d_step1", tag="z_grouped", align_bytes=64),
+            reuse.tile([P, 2, S], F32, name="d_step1", tag="z_planes", align_bytes=64),
         ]
         for t in range(PACK):
             nc.vector.tensor_tensor(d_step[t // 2][:, t % 2, :], d_win[t][:].indirect(n4_t[:]), d_own[t], ALU.subtract)
 
         out_rows = out.rearrange("(p t) j -> p t j", t=PACK)
-        halves = [slice(0, HALF), slice(HALF, S)]
         for pair, spent in enumerate(("z_codes", "w2_codes")):
             tiles = (2 * pair, 2 * pair + 1)
             gate = reuse.tile([P, 2, S], F32, name=f"gate{pair}", tag=spent, align_bytes=64)
@@ -194,7 +204,17 @@ def tile_picked_latepullbhopp_none_p_kernel(
             nc.scalar.activation(gate[:], d_step[pair][:], ACT.Sigmoid)
             for i, t in enumerate(tiles):
                 nc.vector.tensor_tensor(pull[:, i, :], gate[:, i, :], h_step[:, i, :], ALU.mult)
-            for i, t in enumerate(tiles):
-                for cols in halves if t == PACK - 1 else [slice(0, S)]:
-                    nc.vector.tensor_tensor(result[:, i, cols], pull[:, i, cols], h_own[t][:, cols], ALU.add)
-                    nc.sync.dma_start(out_rows[:, t, cols], result[:, i, cols])
+            first, second = tiles
+            nc.gpsimd.tensor_tensor(result[:, 0, :HALF], pull[:, 0, :HALF], h_own[first][:, :HALF], ALU.add)
+            nc.vector.tensor_tensor(result[:, 0, HALF:], pull[:, 0, HALF:], h_bank[first][:, HALF:], ALU.add)
+            if pair == 0:
+                nc.vector.tensor_tensor(result[:, 1, :], pull[:, 1, :], h_bank[second][:], ALU.add)
+                for i, t in enumerate(tiles):
+                    nc.sync.dma_start(out_rows[:, t, :], result[:, i, :])
+            else:
+                nc.sync.dma_start(out_rows[:, first, HALF:], result[:, 0, HALF:])
+                nc.vector.tensor_tensor(result[:, 1, :HALF], pull[:, 1, :HALF], h_bank[second][:, :HALF], ALU.add)
+                nc.sync.dma_start(out_rows[:, second, :HALF], result[:, 1, :HALF])
+                nc.sync.dma_start(out_rows[:, first, :HALF], result[:, 0, :HALF])
+                nc.vector.tensor_tensor(result[:, 1, HALF:], pull[:, 1, HALF:], h_bank[second][:, HALF:], ALU.add)
+                nc.sync.dma_start(out_rows[:, second, HALF:], result[:, 1, HALF:])

from contextlib import ExitStack

import concourse.mybir as mybir

F32 = mybir.dt.float32
BF16 = mybir.dt.bfloat16
I32 = mybir.dt.int32
U32 = mybir.dt.uint32
U16 = mybir.dt.uint16
U8 = mybir.dt.uint8
FP8X4 = mybir.dt.float8_e4m3fn_x4
ALU = mybir.AluOpType
ACT = mybir.ActivationFunctionType

P = 128
PACK = 4
K, T, S = 512, 2048, 512
HALF = S // 2
LIST_COLS = S // 16
FLOPS = 3 * 2 * 512 * 512 * 512


def tile_picked_latepullbhopp_none_p_kernel(
    tc, x_words, x_scales, w1, gn, w2, w3, offs, n1, n2, two, n3, n4, out
):
    nc = tc.nc
    with ExitStack() as ctx:
        lists = ctx.enter_context(tc.tile_pool(name="lists", bufs=1))
        keep = ctx.enter_context(tc.tile_pool(name="keep", bufs=1))
        reuse = ctx.enter_context(tc.tile_pool(name="reuse", bufs=1))
        psum = ctx.enter_context(tc.psum_pool(name="psum", bufs=1))

        def load_list(src, name):
            dst = lists.tile([P, LIST_COLS], U16, name=name)
            nc.sync.dma_start(dst[:], src)
            return dst

        def load_weight(w, c0, c1, name):
            raw = reuse.tile([P, PACK, c1 - c0], F32, name=name, align_bytes=64)
            nc.sync.dma_start(raw[:], w.rearrange("(p j) c -> p j c", j=PACK)[:, :, c0:c1])
            return raw

        def dealt(grouped, raw, c0, c1):
            dst = grouped[:].rearrange("p (t m j) -> p m j t", t=PACK, j=PACK)[:, c0 // PACK : c1 // PACK, :, :]
            return dst, raw[:].rearrange("p j (m t) -> p m j t", t=PACK)

        def chained_windows(name):
            wins = [reuse.tile([P, 2 * S], F32, name=f"{name}_win{t}", align_bytes=64) for t in range(PACK)]
            last = keep.tile([P, S], F32, name=f"{name}_last")
            return wins, [wins[t + 1][:, S:] for t in range(PACK - 1)] + [last[:]]

        table_words = keep.tile([P, T], U32, name="table_words")
        table_bytes = keep.tile([P, T], U8, name="table_bytes")
        nc.gpsimd.memset(table_bytes[:].bitcast(I32), 0)
        gain = keep.tile([P, PACK], F32, name="gain")
        nc.scalar.dma_start(gain[:], gn.rearrange("(p t) o -> p (t o)", t=PACK))
        is_zero = keep.tile([P, PACK], F32, name="is_zero")
        safe_gain = keep.tile([P, PACK], F32, name="safe_gain")
        inv_gain = keep.tile([P, PACK], F32, name="inv_gain")
        nc.vector.tensor_scalar(is_zero[:], gain[:], 0.0, None, ALU.is_equal)
        nc.vector.tensor_tensor(safe_gain[:], gain[:], is_zero[:], ALU.add)
        nc.vector.reciprocal(inv_gain[:], safe_gain[:])
        offs_t = load_list(offs, "offs_t")
        nc.sync.dma_start(table_words[:].bitcast(I32), x_words[0].rearrange("p n r -> p (n r)").bitcast(I32))
        two_t = load_list(two, "two_t")
        for q in range(4):
            nc.sync.dma_start(
                table_bytes[:].bitcast(I32)[32 * q : 32 * q + 4, :], x_scales[0].bitcast(I32)[4 * q : 4 * q + 4, :]
            )
        w1_raw = [load_weight(w1, HALF * a, HALF * (a + 1), f"w1_raw{a}") for a in range(2)]
        w3_raw = [load_weight(w3, 0, HALF, "w3_raw0")]
        n1_t = load_list(n1, "n1_t")
        n2_t = load_list(n2, "n2_t")
        w2_raw = load_weight(w2, 0, S, "w2_raw")
        w3_raw.append(load_weight(w3, HALF, S, "w3_raw1"))
        n4_t = load_list(n4, "n4_t")
        n3_t = load_list(n3, "n3_t")

        y_win, y_own = chained_windows("y")
        tanh_win, st_gain = chained_windows("tanh")
        d_win, d_own = chained_windows("d")
        h_win, h_own = chained_windows("h")
        nc.scalar.activation(y_win[0][:, S:], gain[:, 0:1].to_broadcast([P, S]), ACT.Sigmoid)
        nc.gpsimd.memset(tanh_win[0][:, S:], 0.0)
        nc.gpsimd.memset(d_win[0][:, S:], 0.0)
        nc.gpsimd.memset(h_win[0][:, S:], 0.0)

        x1_words = keep.tile([P, S], U32, name="x1_words", align_bytes=64)
        x1_bytes = keep.tile([P, S], U8, name="x1_bytes", align_bytes=64)
        nc.vector.tensor_copy(x1_words[:], table_words[:].indirect(offs_t[:]))
        x2_words = keep.tile([P, S], U32, name="x2_words", align_bytes=64)
        nc.vector.tensor_copy(x2_words[:], table_words[:].indirect(two_t[:]))
        nc.vector.tensor_copy(x1_bytes[:], table_bytes[:].indirect(offs_t[:]))

        w1_grouped = keep.tile([P, PACK * S], BF16, name="w1_grouped", align_bytes=64)
        for a in range(2):
            dst, src = dealt(w1_grouped, w1_raw[a], HALF * a, HALF * (a + 1))
            nc.scalar.activation(dst, src, ACT.Copy)

        def product(bank, codes, scales, t, words, scale_bytes):
            cols = slice(P * t, P * (t + 1))
            nc.tensor.matmul_mx(
                out=bank,
                lhsT=codes[:, cols].bitcast(FP8X4),
                lhsT_scale=scales[:, cols],
                rhs=words.bitcast(FP8X4),
                rhs_scale=scale_bytes,
                start=True,
                stop=True,
            )

        w1_codes = keep.tile([P, S], U32, name="w1_codes", align_bytes=64)
        w1_scales = keep.tile([P, S], U8, name="w1_scales", align_bytes=64)
        y_bank = [psum.tile([P, S], F32, name=f"y_bank{t}", tag=f"yh{t}") for t in range(PACK)]
        y_spare = psum.tile([P, HALF], F32, name="y_spare", tag="d_bank3")
        y_parts = [[(y_bank[0][:, :HALF], slice(0, HALF)), (y_spare[:], slice(HALF, S))]]
        y_parts.extend([(y_bank[t][:], slice(0, S))] for t in range(1, PACK))
        for t0, t1 in ((0, 1), (1, 2), (2, 4)):
            cols = slice(P * t0, P * t1)
            nc.vector.quantize_mx(
                out=w1_codes[:, cols].bitcast(FP8X4), scales=w1_scales[:, cols], in_=w1_grouped[:, S * t0 : S * t1]
            )
            for t in range(t0, t1):
                for bank, cols in y_parts[t]:
                    product(bank, w1_codes, w1_scales, t, x1_words[:, cols], x1_bytes[:, cols])

        x2_bytes = reuse.tile([P, S], U8, name="x2_bytes", tag="w1_raw1", align_bytes=64)
        nc.vector.tensor_copy(x2_bytes[:], table_bytes[:].indirect(two_t[:]))

        for t in range(PACK):
            for bank, cols in y_parts[t]:
                nc.scalar.activation(y_win[t][:, cols], bank, ACT.Copy, scale=gain[:, t : t + 1])
                nc.scalar.activation(y_own[t][:, cols], bank, ACT.Copy, scale=gain[:, t : t + 1])

        for t in range(PACK):
            nc.vector.tensor_tensor(st_gain[t], y_win[t][:].indirect(n1_t[:]), y_own[t], ALU.add)

        def deal_halves(grouped, raws):
            for a in range(2):
                dst, src = dealt(grouped, raws[a], HALF * a, HALF * (a + 1))
                nc.scalar.activation(dst, src, ACT.Copy)

        def quantise(grouped, name):
            codes = reuse.tile([P, S], U32, name=f"{name}_codes", align_bytes=64)
            scales = reuse.tile([P, S], U8, name=f"{name}_scales", align_bytes=64)
            nc.vector.quantize_mx(out=codes[:].bitcast(FP8X4), scales=scales[:], in_=grouped[:])
            return codes, scales

        w3_grouped = keep.tile([P, PACK * S], BF16, name="w3_grouped", align_bytes=64)
        deal_halves(w3_grouped, w3_raw)
        w3_codes, w3_scales = quantise(w3_grouped, "w3")
        d_bank = [psum.tile([P, S], F32, name=f"d_bank{t}") for t in range(PACK)]
        for t in range(PACK):
            product(d_bank[t][:], w3_codes, w3_scales, t, x2_words[:], x2_bytes[:])

        z_planes = reuse.tile([P, PACK, S], F32, name="z_planes", align_bytes=64)
        for t in range(PACK):
            nc.scalar.activation(tanh_win[t][:, :S], st_gain[t], ACT.Tanh, scale=inv_gain[:, t : t + 1])
            nc.vector.tensor_tensor(z_planes[:, t, :], tanh_win[t][:].indirect(n2_t[:]), st_gain[t], ALU.mult)

        def leave_by_dma(t):
            nc.scalar.copy(d_win[t][:, :S], d_bank[t][:])
            nc.sync.dma_start(d_own[t], d_win[t][:, :S])

        leave_by_dma(0)
        leave_by_dma(1)

        w2_grouped = reuse.tile([P, PACK * S], BF16, name="w2_grouped", tag="y_win0", align_bytes=64)
        w2_dst, w2_src = dealt(w2_grouped, w2_raw, 0, S)
        nc.scalar.activation(w2_dst, w2_src, ACT.Copy)
        leave_by_dma(2)
        z_grouped = keep.tile([P, PACK * S], BF16, name="z_grouped", align_bytes=64)
        nc.scalar.activation(
            z_grouped[:].rearrange("p (c i t) -> p c t i", i=4, t=PACK),
            z_planes[:].rearrange("p t (c i) -> p c t i", i=4),
            ACT.Copy,
        )
        nc.scalar.copy(d_win[3][:, :S], d_bank[3][:])
        nc.scalar.copy(d_own[3], d_bank[3][:])
        w2_codes, w2_scales = quantise(w2_grouped, "w2")
        z_codes, z_scales = quantise(z_grouped, "z")
        h_bank = [psum.tile([P, S], F32, name=f"h_bank{t}", tag=f"yh{t}") for t in range(PACK)]
        for t in range(PACK):
            product(h_bank[t][:], w2_codes, w2_scales, t, z_codes[:], z_scales[:])

        d_step = [
            keep.tile([P, 2, S], F32, name="d_step0"),
            reuse.tile([P, 2, S], F32, name="d_step1", tag="z_planes", align_bytes=64),
        ]
        for t in range(PACK):
            nc.vector.tensor_tensor(d_step[t // 2][:, t % 2, :], d_win[t][:].indirect(n4_t[:]), d_own[t], ALU.subtract)

        out_rows = out.rearrange("(p t) j -> p t j", t=PACK)
        for pair, spent in enumerate(("z_codes", "w2_codes")):
            tiles = (2 * pair, 2 * pair + 1)
            gate = reuse.tile([P, 2, S], F32, name=f"gate{pair}", tag=spent, align_bytes=64)
            h_step = keep.tile([P, 2, S], F32, name=f"h_step{pair}")
            pull = keep.tile([P, 2, S], F32, name=f"pull{pair}")
            result = keep.tile([P, 2, S], F32, name=f"result{pair}")
            for i, t in enumerate(tiles):
                nc.scalar.copy(h_win[t][:, :S], h_bank[t][:])
                nc.scalar.copy(h_own[t], h_bank[t][:])
                nc.vector.tensor_tensor(h_step[:, i, :], h_win[t][:].indirect(n3_t[:]), h_own[t], ALU.subtract)
            nc.scalar.activation(gate[:], d_step[pair][:], ACT.Sigmoid)
            for i, t in enumerate(tiles):
                nc.vector.tensor_tensor(pull[:, i, :], gate[:, i, :], h_step[:, i, :], ALU.mult)
            first, second = tiles
            nc.gpsimd.tensor_tensor(result[:, 0, :HALF], pull[:, 0, :HALF], h_own[first][:, :HALF], ALU.add)
            nc.vector.tensor_tensor(result[:, 0, HALF:], pull[:, 0, HALF:], h_bank[first][:, HALF:], ALU.add)
            if pair == 0:
                nc.vector.tensor_tensor(result[:, 1, :], pull[:, 1, :], h_bank[second][:], ALU.add)
                for i, t in enumerate(tiles):
                    nc.sync.dma_start(out_rows[:, t, :], result[:, i, :])
            else:
                nc.sync.dma_start(out_rows[:, first, HALF:], result[:, 0, HALF:])
                nc.vector.tensor_tensor(result[:, 1, :HALF], pull[:, 1, :HALF], h_bank[second][:, :HALF], ALU.add)
                nc.sync.dma_start(out_rows[:, second, :HALF], result[:, 1, :HALF])
                nc.sync.dma_start(out_rows[:, first, :HALF], result[:, 0, :HALF])
                nc.vector.tensor_tensor(result[:, 1, HALF:], pull[:, 1, HALF:], h_bank[second][:, HALF:], ALU.add)
                nc.sync.dma_start(out_rows[:, second, HALF:], result[:, 1, HALF:])
